import numpy as np
import ml_dtypes


def mxq(x, axis, fmt="e4m3"):
    dtype, down = {"e4m3": (ml_dtypes.float8_e4m3fn, 7), "e5m2": (ml_dtypes.float8_e5m2, 14)}[fmt]
    v = np.moveaxis(np.asarray(x, np.float32).astype(ml_dtypes.bfloat16).astype(np.float64), axis, -1)
    blocks = v.reshape(v.shape[:-1] + (-1, 32))
    amax = np.abs(blocks).max(-1, keepdims=True)
    byte = np.maximum(np.where(amax > 0, np.frexp(amax)[1] - 1 + 127, 0) - down, 1)
    scale = np.exp2(byte - 127.0)
    codes = (blocks / scale).astype(np.float32).astype(dtype).astype(np.float64)
    return np.moveaxis((codes * scale).reshape(v.shape), -1, axis)


WIDE = False


def mx_kscale(k):
    if not WIDE:
        return np.ones(k)
    levels = np.array([10, -10, 5, -5, 0])
    if k % 512:
        return np.exp2(np.random.permutation(np.resize(levels, k // 32))).repeat(32)
    a = np.empty((k // 512, 16))
    for p in range(k // 512):
        a[p, :8] = np.random.permutation(np.resize(levels, 8))
        for g in range(8):
            far = levels[np.abs(levels - a[p, g]) >= 10]
            a[p, g + 8] = far[np.random.randint(len(far))]
    return np.exp2(a.ravel()).repeat(32)


def f64(x):
    return np.asarray(x).astype(np.float64)


def striped(idx):
    return np.tile(idx.reshape(-1, 16).T, (8, 1)).astype(np.uint16)


def unstriped(offs):
    return offs[:16].T.reshape(-1).astype(np.int64)


def striped8(idx):
    return np.concatenate([x.reshape(-1, 16).T for x in idx]).astype(np.uint16)


def runs(offs, k):
    lists = np.stack([offs[16 * r : 16 * r + 16].T.reshape(-1) for r in range(8)]).astype(np.int64)
    return lists[np.arange(k) % 512 // 64]


def pack_weight(w):
    k, n = w.shape
    w = f64(np.asarray(w, np.float32).astype(ml_dtypes.bfloat16)).reshape(k // 32, 32, n)
    amax = np.abs(w).max(1)
    byte = np.clip(np.where(amax > 0, np.frexp(amax)[1] - 1 + 127 - 7, 1), 1, 254)
    scaled = (w * np.exp2(127.0 - byte)[:, None, :]).reshape(k, n).astype(np.float32)
    words = np.ascontiguousarray(scaled.reshape(k // 512, 128, 4, n).transpose(0, 1, 3, 2)).astype(ml_dtypes.float8_e4m3fn).view(np.uint8)
    return words, np.ascontiguousarray(byte.astype(np.uint8).reshape(k // 512, 16, n))


def unpack_weight(words, scales):
    g, p, n, _ = words.shape
    vals = np.ascontiguousarray(words).view(ml_dtypes.float8_e4m3fn).astype(np.float64) * np.repeat(np.exp2(scales.astype(np.float64) - 127.0), 8, axis=1)[..., None]
    return vals.transpose(0, 1, 3, 2).reshape(g * 512, n)


K, T, S, V, H, W = 512, 2048, 512, 512, 512, 256


def setup_inputs():
    n = np.random.standard_normal
    s = mx_kscale(K)[:, None]
    u = mx_kscale(S)
    packed_xT = pack_weight(n((K, T)) * s)
    perm = np.stack([np.random.permutation(V) for _ in range(8)])
    return {
        "x_words": packed_xT[0],
        "x_scales": packed_xT[1],
        "w1": (n((K, H)) / np.sqrt(K) / s).astype(np.float32),
        "w2": (n((K, H)) / np.sqrt(K) / s).astype(np.float32),
        "ga": (np.random.uniform(0.5, 1.5, (H, 1)) * u[:, None]).astype(np.float32),
        "gb": (np.random.uniform(0.5, 1.5, (H, 1)) / u[:, None]).astype(np.float32),
        "offs": striped(np.random.permutation(T)[:S]),
        "two": striped(np.random.permutation(T)[:V]),
        "n1": striped8(np.stack([np.random.permutation(S) for _ in range(8)])),
        "n2": striped8(np.stack([np.random.permutation(V) for _ in range(8)])),
        "n3": striped8(np.stack([np.random.permutation(V) for _ in range(8)])),
        "n4": striped8(np.stack([np.random.permutation(V) for _ in range(8)])),
        "n5": striped8(perm[:, :W]),
        "n6": striped8(perm[:, W:]),
        "n7": striped8(np.stack([np.random.permutation(V) for _ in range(8)])),
    }


def reference(x_words, x_scales, w1, w2, ga, gb, offs, two, n1, n2, n3, n4, n5, n6, n7):
    xq = unpack_weight(x_words, x_scales)[:, unstriped(offs)]
    a = mxq(f64(w1), 0, "e4m3").T @ xq
    z = f64(ga) * (np.maximum(a, a[np.arange(H)[:, None], runs(n1, H)]))
    x_two = unpack_weight(x_words, x_scales)[:, unstriped(two)]
    b = mxq(f64(w2), 0, "e4m3").T @ x_two
    z2 = f64(gb) * (b + b[np.arange(H)[:, None], runs(n2, H)] - (np.maximum(b[np.arange(H)[:, None], runs(n3, H)], b[np.arange(H)[:, None], runs(n4, H)])))
    s = 0.0625 * ((mxq(z, 0, "e4m3").T @ mxq(z2, 0, "e4m3")))
    pa = s[np.arange(S)[:, None], runs(n5, S)]
    pb = s[np.arange(S)[:, None], runs(n6, S)]
    ra = pa - (0.5 * pb)
    ds = s.copy()
    ds[np.arange(S)[:, None], runs(n6, S)] = ra
    return ds - (0.5 * (ds[np.arange(S)[:, None], runs(n7, S)]))

@@ -1,0 +1,237 @@
+from contextlib import ExitStack
+
+import concourse.mybir as mybir
+
+K, T, S, V, H, W = 512, 2048, 512, 512, 512, 256
+FLOPS = 2 * K * H * S + 2 * K * H * V + 2 * H * S * V
+
+F32 = mybir.dt.float32
+BF16 = mybir.dt.bfloat16
+I32 = mybir.dt.int32
+U32 = mybir.dt.uint32
+U16 = mybir.dt.uint16
+U8 = mybir.dt.uint8
+FP8X4 = mybir.dt.float8_e4m3fn_x4
+ALU = mybir.AluOpType
+ACT = mybir.ActivationFunctionType
+
+P = 128
+PACK = 4
+WIN = 1024
+
+
+def tile_picked_kqbigtrimfoldd_none_p_kernel(tc, x_words, x_scales, w1, w2, ga, gb, offs, two, n1, n2, n3, n4, n5, n6, n7, out):
+    nc = tc.nc
+    with ExitStack() as ctx:
+        keep = ctx.enter_context(tc.tile_pool(name="keep", bufs=1))
+        ring = ctx.enter_context(tc.tile_pool(name="ring", bufs=2))
+        psum = ctx.enter_context(tc.psum_pool(name="psum", bufs=1))
+
+        def load_list(name, src):
+            held = keep.tile([P, src.shape[1]], U16, name=name)
+            nc.sync.dma_start(held[:], src)
+            return held
+
+        xs = keep.tile([P, T], U8, name="xs", align_bytes=64)
+        nc.vector.memset(xs[:].bitcast(I32), 0)
+        for q in range(4):
+            nc.scalar.dma_start(xs[32 * q : 32 * q + 4, :].bitcast(I32), x_scales[0, 4 * q : 4 * q + 4, :].bitcast(I32))
+        l_two = load_list("l_two", two)
+        l_offs = load_list("l_offs", offs)
+        xw = keep.tile([P, T], U32, name="xw", align_bytes=64)
+        nc.sync.dma_start(xw[:].bitcast(I32), x_words[0].rearrange("p n t -> p (n t)").bitcast(I32))
+        w2_raw = keep.tile([P, PACK, H], F32, name="w2_raw")
+        nc.sync.dma_start(w2_raw[:], w2.rearrange("(p j) c -> p j c", j=PACK))
+        ga_t = keep.tile([P, PACK], F32, name="ga_t")
+        nc.sync.dma_start(ga_t[:], ga.rearrange("(p t) o -> p (t o)", t=PACK))
+        w1_raw = keep.tile([P, PACK, H], F32, name="w1_raw")
+        nc.sync.dma_start(w1_raw[:], w1.rearrange("(p j) c -> p j c", j=PACK))
+        l3 = load_list("l3", n3)
+        l4 = load_list("l4", n4)
+        l2 = load_list("l2", n2)
+        gb_t = keep.tile([P, PACK], F32, name="gb_t")
+        nc.sync.dma_start(gb_t[:], gb.rearrange("(p t) o -> p (t o)", t=PACK))
+        l1 = load_list("l1", n1)
+        l5 = load_list("l5", n5)
+        l6 = load_list("l6", n6)
+        l7 = load_list("l7", n7)
+
+        win_b = [keep.tile([P, WIN], F32, name="win_b%d" % j) for j in range(PACK)]
+        win_a = [keep.tile([P, WIN], F32, name="win_a%d" % j) for j in range(PACK)]
+        for w in win_b + win_a:
+            nc.gpsimd.memset(w[:, V:], 0.0)
+
+        ga_abs = keep.tile([P, PACK], F32, name="ga_abs")
+        nc.scalar.activation(ga_abs[:], ga_t[:], ACT.Abs)
+        ga_pos = keep.tile([P, PACK], F32, name="ga_pos")
+        nc.gpsimd.tensor_scalar(ga_pos[:], ga_t[:], 0.0, 2.0, ALU.is_ge, ALU.mult)
+        ga_sign = keep.tile([P, PACK], F32, name="ga_sign")
+        nc.gpsimd.tensor_scalar(ga_sign[:], ga_pos[:], -1.0, 1.0, ALU.add, ALU.mult)
+        gb_signed = keep.tile([P, PACK], F32, name="gb_signed")
+        nc.gpsimd.tensor_tensor(gb_signed[:], gb_t[:], ga_sign[:], ALU.mult)
+
+        def pick_scales(name, lst):
+            scales = keep.tile([P, S], U8, name=name + "_scales", align_bytes=64)
+            nc.vector.tensor_copy(scales[:], xs[:].indirect(lst[:]))
+            return scales
+
+        def pick_words(name, lst):
+            words = keep.tile([P, S], U32, name=name, align_bytes=64)
+            nc.vector.tensor_copy(words[:], xw[:].indirect(lst[:]))
+            return words
+
+        def deal(name, src, ts, on_vector):
+            grouped = keep.tile([P, len(ts) * P * PACK], BF16, name=name + "_grouped", align_bytes=64)
+            for i, t in enumerate(ts):
+                dst = grouped[:, i * P * PACK : (i + 1) * P * PACK].rearrange("p (m j) -> p m j", j=PACK)
+                view = src[:].rearrange("p j (m t) -> p t m j", t=PACK)[:, t]
+                if on_vector:
+                    nc.vector.tensor_copy(dst, view)
+                else:
+                    nc.scalar.copy(dst, view)
+            return grouped
+
+        def quantise(name, grouped):
+            width = grouped.shape[1] // PACK
+            words = keep.tile([P, width], U32, name=name + "_words", align_bytes=64)
+            scales = keep.tile([P, width], U8, name=name + "_scales", align_bytes=64)
+            nc.vector.quantize_mx(out=words[:].bitcast(FP8X4), scales=scales[:], in_=grouped[:])
+            return words, scales
+
+        def product(bank, stationary, col, moving):
+            acc = psum.tile([P, V], F32, name="bank%d" % bank)
+            cols = slice(col * P, (col + 1) * P)
+            nc.tensor.matmul_mx(out=acc[:], lhsT=stationary[0][:, cols].bitcast(FP8X4), lhsT_scale=stationary[1][:, cols],
+                                rhs=moving[0][:].bitcast(FP8X4), rhs_scale=moving[1][:], start=True, stop=True)
+            return acc
+
+        xb_scales = pick_scales("xb", l_two)
+        x_b = (pick_words("xb_words", l_two), xb_scales)
+        xa_scales = pick_scales("xa", l_offs)
+
+        b_plain = [keep.tile([P, V], F32, name="b_plain%d" % j) for j in range(PACK)]
+
+        def b_rows(j, stationary, col):
+            acc = product(j, stationary, col, x_b)
+            nc.scalar.copy(win_b[j][:, :V], acc[:])
+            nc.scalar.copy(b_plain[j][:], acc[:])
+
+        w2q0 = quantise("w2q0", deal("w2g0", w2_raw, [0], True))
+        x_a = (pick_words("w2g0_grouped", l_offs), xa_scales)
+        w2g1 = deal("w2g1", w2_raw, [1], False)
+        b_rows(0, w2q0, 0)
+        w2q1 = quantise("w2q1", w2g1)
+        b_rows(1, w2q1, 0)
+        w2q2 = quantise("w2q2", deal("w2g2", w2_raw, [2, 3], False))
+        b_rows(2, w2q2, 0)
+        b_rows(3, w2q2, 1)
+
+        z2_rows = keep.tile([P, PACK, V], BF16, name="z2_rows")
+        z_rows = keep.tile([P, PACK, S], BF16, name="z_rows")
+        d3 = {}
+        d4 = {}
+        top = {}
+        a_acc = {}
+        a_got = {}
+
+        def b_first(j):
+            d3[j] = ring.tile([P, V], F32, name="d3")
+            nc.vector.tensor_tensor(d3[j][:], win_b[j][:].indirect(l3[:]), b_plain[j][:], ALU.subtract)
+
+        def b_second(j):
+            d4[j] = ring.tile([P, V], F32, name="d4")
+            nc.vector.tensor_tensor(d4[j][:], win_b[j][:].indirect(l4[:]), b_plain[j][:], ALU.subtract)
+
+        def b_top(j):
+            top[j] = ring.tile([P, V], F32, name="top")
+            nc.vector.tensor_tensor(top[j][:], d3[j][:], d4[j][:], ALU.max)
+
+        def b_last(j):
+            z2f = ring.tile([P, V], F32, name="z2f")
+            nc.vector.tensor_tensor(z2f[:], win_b[j][:].indirect(l2[:]), top[j][:], ALU.subtract)
+            nc.scalar.activation(z2_rows[:, j, :], z2f[:], ACT.Copy, scale=gb_signed[:, j : j + 1])
+
+        def a_rows(j, stationary):
+            a_acc[j] = product(PACK + j, stationary, j, x_a)
+            nc.scalar.activation(win_a[j][:, :S], a_acc[j][:], ACT.Copy, scale=ga_abs[:, j : j + 1])
+
+        def a_gather(j):
+            a_got[j] = ring.tile([P, S], F32, name="a_got")
+            nc.vector.tensor_copy(a_got[j][:], win_a[j][:].indirect(l1[:]))
+
+        def a_top(j):
+            nc.vector.scalar_tensor_tensor(z_rows[:, j, :], a_acc[j][:], ga_abs[:, j : j + 1], a_got[j][:], ALU.mult, ALU.max)
+
+        b_first(0)
+        b_second(0)
+        for j in range(1, PACK):
+            b_first(j)
+            b_top(j - 1)
+            b_second(j)
+            b_last(j - 1)
+            if j == 2:
+                w1q = quantise("w1q", deal("w1g", w1_raw, [0, 1, 2, 3], False))
+                for i in range(PACK):
+                    a_rows(i, w1q)
+        a_gather(0)
+        b_top(3)
+        a_gather(1)
+        b_last(3)
+        z2_grouped = keep.tile([P, V * PACK], BF16, name="z2_grouped", align_bytes=64)
+        nc.scalar.copy(z2_grouped[:].rearrange("p (v j) -> p v j", j=PACK), z2_rows[:].rearrange("p j v -> p v j"))
+        a_top(0)
+        a_gather(2)
+        a_top(1)
+        a_gather(3)
+        a_top(2)
+        z2q = quantise("z2q", z2_grouped)
+        a_top(3)
+
+        zg = [deal("zg%d" % t, z_rows, [t], True) for t in range(2)]
+        out_rows = out.rearrange("(p t) v -> t p v", t=PACK)
+
+        def s_rows(t):
+            acc = product(t, quantise("zq%d" % t, zg[t]), 0, z2q)
+            nc.scalar.activation(win_b[t][:, :V], acc[:], ACT.Copy, scale=0.0625)
+
+        s_rows(0)
+        zg.append(deal("zg2", z_rows, [2], True))
+        s_rows(1)
+        zg.append(deal("zg3", z_rows, [3], True))
+        s_rows(2)
+        s_rows(3)
+
+        pa = {}
+        pb = {}
+
+        def pair_up(t):
+            pa[t] = ring.tile([P, W], F32, name="pa")
+            nc.vector.tensor_copy(pa[t][:], win_b[t][:].indirect(l5[:]))
+            pb[t] = ring.tile([P, W], F32, name="pb")
+            nc.vector.tensor_scalar(pb[t][:], win_b[t][:].indirect(l6[:]), -0.5, 0.0, ALU.mult, ALU.add)
+
+        def put_back(t):
+            nc.vector.tensor_tensor(win_b[t][:].indirect(l6[:]), pa[t][:], pb[t][:], ALU.add)
+            nc.scalar.activation(win_a[t][:, :V], win_b[t][:, :V], ACT.Copy, scale=-0.5)
+
+        def finish(t, pieces):
+            width = V // pieces
+            for i in range(pieces):
+                cols = slice(i * width, (i + 1) * width)
+                res = keep.tile([P, width], F32, name="res%d_%d" % (t, i))
+                entries = l7[:, i * width // 16 : (i + 1) * width // 16]
+                nc.vector.tensor_tensor(res[:], win_a[t][:].indirect(entries), win_b[t][:, cols], ALU.add)
+                nc.sync.dma_start(out_rows[t][:, cols], res[:])
+
+        pair_up(0)
+        pair_up(1)
+        put_back(0)
+        pair_up(2)
+        put_back(1)
+        finish(0, 1)
+        pair_up(3)
+        put_back(2)
+        finish(1, 1)
+        put_back(3)
+        finish(2, 1)
+        finish(3, 2)

@@ -18,6 +18,7 @@ ACT = mybir.ActivationFunctionType
 P = 128
 PACK = 4
 WIN = 1024
+HALF = V // 2
 
 
 def tile_picked_kqbigtrimfoldd_none_p_kernel(tc, x_words, x_scales, w1, w2, ga, gb, offs, two, n1, n2, n3, n4, n5, n6, n7, out):
@@ -32,25 +33,31 @@ def tile_picked_kqbigtrimfoldd_none_p_kernel(tc, x_words, x_scales, w1, w2, ga, 
             nc.sync.dma_start(held[:], src)
             return held
 
+        def load_weight(name, src):
+            held = keep.tile([P, PACK, H], F32, name=name)
+            nc.sync.dma_start(held[:], src.rearrange("(p j) c -> p j c", j=PACK))
+            return held
+
+        def load_gain(name, src):
+            held = keep.tile([P, PACK], F32, name=name)
+            nc.sync.dma_start(held[:], src.rearrange("(p t) o -> p (t o)", t=PACK))
+            return held
+
         xs = keep.tile([P, T], U8, name="xs", align_bytes=64)
-        nc.vector.memset(xs[:].bitcast(I32), 0)
+        nc.gpsimd.memset(xs[:].bitcast(I32), 0)
         for q in range(4):
             nc.scalar.dma_start(xs[32 * q : 32 * q + 4, :].bitcast(I32), x_scales[0, 4 * q : 4 * q + 4, :].bitcast(I32))
         l_two = load_list("l_two", two)
         l_offs = load_list("l_offs", offs)
+        w2_raw = load_weight("w2_raw", w2)
         xw = keep.tile([P, T], U32, name="xw", align_bytes=64)
         nc.sync.dma_start(xw[:].bitcast(I32), x_words[0].rearrange("p n t -> p (n t)").bitcast(I32))
-        w2_raw = keep.tile([P, PACK, H], F32, name="w2_raw")
-        nc.sync.dma_start(w2_raw[:], w2.rearrange("(p j) c -> p j c", j=PACK))
-        ga_t = keep.tile([P, PACK], F32, name="ga_t")
-        nc.sync.dma_start(ga_t[:], ga.rearrange("(p t) o -> p (t o)", t=PACK))
-        w1_raw = keep.tile([P, PACK, H], F32, name="w1_raw")
-        nc.sync.dma_start(w1_raw[:], w1.rearrange("(p j) c -> p j c", j=PACK))
+        ga_t = load_gain("ga_t", ga)
         l3 = load_list("l3", n3)
         l4 = load_list("l4", n4)
         l2 = load_list("l2", n2)
-        gb_t = keep.tile([P, PACK], F32, name="gb_t")
-        nc.sync.dma_start(gb_t[:], gb.rearrange("(p t) o -> p (t o)", t=PACK))
+        w1_raw = load_weight("w1_raw", w1)
+        gb_t = load_gain("gb_t", gb)
         l1 = load_list("l1", n1)
         l5 = load_list("l5", n5)
         l6 = load_list("l6", n6)
@@ -58,7 +65,7 @@ def tile_picked_kqbigtrimfoldd_none_p_kernel(tc, x_words, x_scales, w1, w2, ga, 
 
         win_b = [keep.tile([P, WIN], F32, name="win_b%d" % j) for j in range(PACK)]
         win_a = [keep.tile([P, WIN], F32, name="win_a%d" % j) for j in range(PACK)]
-        for w in win_b + win_a:
+        for w in win_b:
             nc.gpsimd.memset(w[:, V:], 0.0)
 
         ga_abs = keep.tile([P, PACK], F32, name="ga_abs")
@@ -70,63 +77,56 @@ def tile_picked_kqbigtrimfoldd_none_p_kernel(tc, x_words, x_scales, w1, w2, ga, 
         gb_signed = keep.tile([P, PACK], F32, name="gb_signed")
         nc.gpsimd.tensor_tensor(gb_signed[:], gb_t[:], ga_sign[:], ALU.mult)
 
-        def pick_scales(name, lst):
-            scales = keep.tile([P, S], U8, name=name + "_scales", align_bytes=64)
-            nc.vector.tensor_copy(scales[:], xs[:].indirect(lst[:]))
-            return scales
+        def mx_tiles(name, width):
+            return (keep.tile([P, width], U32, name=name + "_words", align_bytes=64),
+                    keep.tile([P, width], U8, name=name + "_scales", align_bytes=64))
 
-        def pick_words(name, lst):
-            words = keep.tile([P, S], U32, name=name, align_bytes=64)
-            nc.vector.tensor_copy(words[:], xw[:].indirect(lst[:]))
-            return words
-
-        def deal(name, src, ts, on_vector):
-            grouped = keep.tile([P, len(ts) * P * PACK], BF16, name=name + "_grouped", align_bytes=64)
-            for i, t in enumerate(ts):
-                dst = grouped[:, i * P * PACK : (i + 1) * P * PACK].rearrange("p (m j) -> p m j", j=PACK)
-                view = src[:].rearrange("p j (m t) -> p t m j", t=PACK)[:, t]
-                if on_vector:
-                    nc.vector.tensor_copy(dst, view)
-                else:
-                    nc.scalar.copy(dst, view)
+        def deal(copy, name, src, t, m0, m1):
+            grouped = keep.tile([P, (m1 - m0) * PACK], BF16, name=name, align_bytes=64)
+            copy(grouped[:].rearrange("p (m j) -> p m j", j=PACK), src[:].rearrange("p j (m t) -> p t m j", t=PACK)[:, t, m0:m1])
             return grouped
 
-        def quantise(name, grouped):
-            width = grouped.shape[1] // PACK
-            words = keep.tile([P, width], U32, name=name + "_words", align_bytes=64)
-            scales = keep.tile([P, width], U8, name=name + "_scales", align_bytes=64)
-            nc.vector.quantize_mx(out=words[:].bitcast(FP8X4), scales=scales[:], in_=grouped[:])
-            return words, scales
+        def quantise(held, col, grouped):
+            cols = slice(col, col + grouped.shape[1] // PACK)
+            nc.vector.quantize_mx(out=held[0][:, cols].bitcast(FP8X4), scales=held[1][:, cols], in_=grouped[:])
 
-        def product(bank, stationary, col, moving):
-            acc = psum.tile([P, V], F32, name="bank%d" % bank)
-            cols = slice(col * P, (col + 1) * P)
-            nc.tensor.matmul_mx(out=acc[:], lhsT=stationary[0][:, cols].bitcast(FP8X4), lhsT_scale=stationary[1][:, cols],
-                                rhs=moving[0][:].bitcast(FP8X4), rhs_scale=moving[1][:], start=True, stop=True)
+        def product(bank, stationary, moving, cols):
+            acc = psum.tile([P, cols.stop - cols.start], F32, name="bank%d" % bank)
+            nc.tensor.matmul_mx(out=acc[:], lhsT=stationary[0][:].bitcast(FP8X4), lhsT_scale=stationary[1][:],
+                                rhs=moving[0][:, cols].bitcast(FP8X4), rhs_scale=moving[1][:, cols], start=True, stop=True)
             return acc
 
-        xb_scales = pick_scales("xb", l_two)
-        x_b = (pick_words("xb_words", l_two), xb_scales)
-        xa_scales = pick_scales("xa", l_offs)
+        halves = [slice(0, HALF), slice(HALF, V)]
+        whole = slice(0, V)
 
-        b_plain = [keep.tile([P, V], F32, name="b_plain%d" % j) for j in range(PACK)]
+        x_b = mx_tiles("xb", V)
+        x_a = mx_tiles("xa", S)
+        nc.vector.tensor_copy(x_b[1][:], xs[:].indirect(l_two[:]))
+        w2q = [mx_tiles("w2q%d" % t, P) for t in range(PACK)]
+        w2g = [deal(nc.vector.tensor_copy, "w2g0", w2_raw, 0, 0, P)]
+        w2g.extend(deal(nc.scalar.copy, "w2g%d" % t, w2_raw, t, 0, P) for t in range(1, PACK))
+        nc.vector.tensor_copy(x_a[1][:], xs[:].indirect(l_offs[:]))
+        quantise(w2q[0], 0, w2g[0])
+        quantise(w2q[1], 0, w2g[1])
+        for cols in halves:
+            nc.vector.tensor_copy(x_b[0][:, cols], xw[:].indirect(l_two[:, cols.start // 16 : cols.stop // 16]))
+        nc.vector.tensor_copy(x_a[0][:], xw[:].indirect(l_offs[:]))
+        quantise(w2q[2], 0, w2g[2])
+        quantise(w2q[3], 0, w2g[3])
 
-        def b_rows(j, stationary, col):
-            acc = product(j, stationary, col, x_b)
-            nc.scalar.copy(win_b[j][:, :V], acc[:])
-            nc.scalar.copy(b_plain[j][:], acc[:])
+        def b_rows(j, bank, cols):
+            acc = product(bank, w2q[j], x_b, cols)
+            nc.scalar.copy(win_b[j][:, cols], acc[:])
+            nc.scalar.copy(win_a[j][:, V + cols.start : V + cols.stop], acc[:])
 
-        w2q0 = quantise("w2q0", deal("w2g0", w2_raw, [0], True))
-        x_a = (pick_words("w2g0_grouped", l_offs), xa_scales)
-        w2g1 = deal("w2g1", w2_raw, [1], False)
-        b_rows(0, w2q0, 0)
-        w2q1 = quantise("w2q1", w2g1)
-        b_rows(1, w2q1, 0)
-        w2q2 = quantise("w2q2", deal("w2g2", w2_raw, [2, 3], False))
-        b_rows(2, w2q2, 0)
-        b_rows(3, w2q2, 1)
+        b_rows(0, 0, halves[0])
+        b_rows(0, PACK, halves[1])
+        for j in range(1, PACK):
+            b_rows(j, j, whole)
 
-        z2_rows = keep.tile([P, PACK, V], BF16, name="z2_rows")
+        z2_rows = keep.tile([P, PACK - 1, V], BF16, name="z2_rows")
+        z2_grouped = keep.tile([P, V * PACK], BF16, name="z2_grouped", align_bytes=64)
+        z2_slots = z2_grouped[:].rearrange("p (v j) -> p v j", j=PACK)
         z_rows = keep.tile([P, PACK, S], BF16, name="z_rows")
         d3 = {}
         d4 = {}
@@ -136,11 +136,11 @@ def tile_picked_kqbigtrimfoldd_none_p_kernel(tc, x_words, x_scales, w1, w2, ga, 
 
         def b_first(j):
             d3[j] = ring.tile([P, V], F32, name="d3")
-            nc.vector.tensor_tensor(d3[j][:], win_b[j][:].indirect(l3[:]), b_plain[j][:], ALU.subtract)
+            nc.vector.tensor_tensor(d3[j][:], win_b[j][:].indirect(l3[:]), win_a[j][:, V:], ALU.subtract)
 
         def b_second(j):
             d4[j] = ring.tile([P, V], F32, name="d4")
-            nc.vector.tensor_tensor(d4[j][:], win_b[j][:].indirect(l4[:]), b_plain[j][:], ALU.subtract)
+            nc.vector.tensor_tensor(d4[j][:], win_b[j][:].indirect(l4[:]), win_a[j][:, V:], ALU.subtract)
 
         def b_top(j):
             top[j] = ring.tile([P, V], F32, name="top")
@@ -149,18 +149,22 @@ def tile_picked_kqbigtrimfoldd_none_p_kernel(tc, x_words, x_scales, w1, w2, ga, 
         def b_last(j):
             z2f = ring.tile([P, V], F32, name="z2f")
             nc.vector.tensor_tensor(z2f[:], win_b[j][:].indirect(l2[:]), top[j][:], ALU.subtract)
-            nc.scalar.activation(z2_rows[:, j, :], z2f[:], ACT.Copy, scale=gb_signed[:, j : j + 1])
+            dst = z2_rows[:, j, :] if j < PACK - 1 else z2_slots[:, :, j]
+            nc.scalar.activation(dst, z2f[:], ACT.Copy, scale=gb_signed[:, j : j + 1])
 
         def a_rows(j, stationary):
-            a_acc[j] = product(PACK + j, stationary, j, x_a)
+            a_acc[j] = product(PACK + j, stationary, x_a, whole)
             nc.scalar.activation(win_a[j][:, :S], a_acc[j][:], ACT.Copy, scale=ga_abs[:, j : j + 1])
 
         def a_gather(j):
             a_got[j] = ring.tile([P, S], F32, name="a_got")
             nc.vector.tensor_copy(a_got[j][:], win_a[j][:].indirect(l1[:]))
 
-        def a_top(j):
-            nc.vector.scalar_tensor_tensor(z_rows[:, j, :], a_acc[j][:], ga_abs[:, j : j + 1], a_got[j][:], ALU.mult, ALU.max)
+        def a_top(j, cols):
+            nc.vector.scalar_tensor_tensor(z_rows[:, j, cols], a_acc[j][:, cols], ga_abs[:, j : j + 1], a_got[j][:, cols], ALU.mult, ALU.max)
+
+        w1g = keep.tile([P, H * PACK], BF16, name="w1g", align_bytes=64)
+        w1q = mx_tiles("w1q", H)
 
         b_first(0)
         b_second(0)
@@ -169,40 +173,53 @@ def tile_picked_kqbigtrimfoldd_none_p_kernel(tc, x_words, x_scales, w1, w2, ga, 
             b_top(j - 1)
             b_second(j)
             b_last(j - 1)
+            if j == 1:
+                for t in range(PACK):
+                    nc.scalar.copy(w1g[:, t * H : (t + 1) * H].rearrange("p (m j) -> p m j", j=PACK), w1_raw[:].rearrange("p j (m t) -> p t m j", t=PACK)[:, t])
             if j == 2:
-                w1q = quantise("w1q", deal("w1g", w1_raw, [0, 1, 2, 3], False))
+                quantise(w1q, 0, w1g)
                 for i in range(PACK):
-                    a_rows(i, w1q)
+                    a_rows(i, (w1q[0][:, i * P : (i + 1) * P], w1q[1][:, i * P : (i + 1) * P]))
+        nc.scalar.copy(z2_slots[:, :, : PACK - 1], z2_rows[:].rearrange("p j v -> p v j"))
         a_gather(0)
         b_top(3)
         a_gather(1)
         b_last(3)
-        z2_grouped = keep.tile([P, V * PACK], BF16, name="z2_grouped", align_bytes=64)
-        nc.scalar.copy(z2_grouped[:].rearrange("p (v j) -> p v j", j=PACK), z2_rows[:].rearrange("p j v -> p v j"))
-        a_top(0)
+        a_top(0, whole)
         a_gather(2)
-        a_top(1)
+        a_top(1, whole)
+        z2q = mx_tiles("z2q", V)
+        quantise(z2q, 0, z2_grouped)
         a_gather(3)
-        a_top(2)
-        z2q = quantise("z2q", z2_grouped)
-        a_top(3)
+        a_top(2, whole)
+        for cols in halves:
+            a_top(3, cols)
 
-        zg = [deal("zg%d" % t, z_rows, [t], True) for t in range(2)]
+        zq = [mx_tiles("zq%d" % t, P) for t in range(PACK)]
+        first = [deal(nc.vector.tensor_copy, "zg0_%d" % h, z_rows, 0, h * P // 2, (h + 1) * P // 2) for h in range(2)]
+        zg3 = deal(nc.scalar.copy, "zg3", z_rows, 3, 0, P)
+        for h in range(2):
+            quantise(zq[0], h * P // 2, first[h])
+        zg1 = deal(nc.vector.tensor_copy, "zg1", z_rows, 1, 0, P)
+        zg2 = deal(nc.vector.tensor_copy, "zg2", z_rows, 2, 0, P)
+        quantise(zq[1], 0, zg1)
+        quantise(zq[2], 0, zg2)
+        quantise(zq[3], 0, zg3)
+
         out_rows = out.rearrange("(p t) v -> t p v", t=PACK)
-
-        def s_rows(t):
-            acc = product(t, quantise("zq%d" % t, zg[t]), 0, z2q)
-            nc.scalar.activation(win_b[t][:, :V], acc[:], ACT.Copy, scale=0.0625)
-
-        s_rows(0)
-        zg.append(deal("zg2", z_rows, [2], True))
-        s_rows(1)
-        zg.append(deal("zg3", z_rows, [3], True))
-        s_rows(2)
-        s_rows(3)
-
+        ds = [keep.tile([P, V], F32, name="ds%d" % t) for t in range(PACK)]
+        s_acc = {}
         pa = {}
         pb = {}
+
+        def s_rows(t, pieces):
+            s_acc[t] = [(cols, product(bank, zq[t], z2q, cols)) for bank, cols in pieces]
+            for cols, acc in s_acc[t]:
+                nc.scalar.activation(win_b[t][:, cols], acc[:], ACT.Copy, scale=0.0625)
+
+        def ds_base(t):
+            for cols, acc in s_acc[t]:
+                nc.scalar.activation(ds[t][:, cols], acc[:], ACT.Copy, scale=0.0625)
 
         def pair_up(t):
             pa[t] = ring.tile([P, W], F32, name="pa")
@@ -211,27 +228,31 @@ def tile_picked_kqbigtrimfoldd_none_p_kernel(tc, x_words, x_scales, w1, w2, ga, 
             nc.vector.tensor_scalar(pb[t][:], win_b[t][:].indirect(l6[:]), -0.5, 0.0, ALU.mult, ALU.add)
 
         def put_back(t):
-            nc.vector.tensor_tensor(win_b[t][:].indirect(l6[:]), pa[t][:], pb[t][:], ALU.add)
-            nc.scalar.activation(win_a[t][:, :V], win_b[t][:, :V], ACT.Copy, scale=-0.5)
+            nc.vector.tensor_tensor(ds[t][:].indirect(l6[:]), pa[t][:], pb[t][:], ALU.add)
+
+        def halve(t):
+            nc.scalar.activation(win_a[t][:, :V], ds[t][:], ACT.Copy, scale=-0.5)
 
         def finish(t, pieces):
-            width = V // pieces
-            for i in range(pieces):
-                cols = slice(i * width, (i + 1) * width)
-                res = keep.tile([P, width], F32, name="res%d_%d" % (t, i))
-                entries = l7[:, i * width // 16 : (i + 1) * width // 16]
-                nc.vector.tensor_tensor(res[:], win_a[t][:].indirect(entries), win_b[t][:, cols], ALU.add)
+            for cols in pieces:
+                res = keep.tile([P, cols.stop - cols.start], F32, name="res%d_%d" % (t, cols.start))
+                entries = l7[:, cols.start // 16 : cols.stop // 16]
+                nc.vector.tensor_tensor(res[:], win_a[t][:].indirect(entries), ds[t][:, cols], ALU.add)
                 nc.sync.dma_start(out_rows[t][:, cols], res[:])
 
+        s_rows(0, [(0, halves[0]), (PACK, halves[1])])
         pair_up(0)
-        pair_up(1)
-        put_back(0)
-        pair_up(2)
-        put_back(1)
-        finish(0, 1)
-        pair_up(3)
-        put_back(2)
-        finish(1, 1)
+        for t in range(1, PACK):
+            s_rows(t, [(t, whole)])
+            ds_base(t - 1)
+            pair_up(t)
+            put_back(t - 1)
+            if t >= 2:
+                halve(t - 2)
+                finish(t - 2, [whole])
+        ds_base(3)
         put_back(3)
-        finish(2, 1)
-        finish(3, 2)
+        halve(2)
+        finish(2, [whole])
+        halve(3)
+        finish(3, halves)

@@ -1,6 +1,7 @@
 from contextlib import ExitStack
 
 import concourse.mybir as mybir
+from concourse.masks import make_identity
 
 K, T, S, V, H, W = 512, 2048, 512, 512, 512, 256
 FLOPS = 2 * K * H * S + 2 * K * H * V + 2 * H * S * V
@@ -19,13 +20,14 @@ P = 128
 PACK = 4
 WIN = 1024
 HALF = V // 2
+SUMMED_ON_TENSOR = 0
 
 
 def tile_picked_kqbigtrimfoldd_none_p_kernel(tc, x_words, x_scales, w1, w2, ga, gb, offs, two, n1, n2, n3, n4, n5, n6, n7, out):
     nc = tc.nc
     with ExitStack() as ctx:
         keep = ctx.enter_context(tc.tile_pool(name="keep", bufs=1))
-        ring = ctx.enter_context(tc.tile_pool(name="ring", bufs=2))
+        ring = ctx.enter_context(tc.tile_pool(name="ring", bufs=4))
         psum = ctx.enter_context(tc.psum_pool(name="psum", bufs=1))
 
         def load_list(name, src):
@@ -68,12 +70,15 @@ def tile_picked_kqbigtrimfoldd_none_p_kernel(tc, x_words, x_scales, w1, w2, ga, 
         for w in win_b:
             nc.gpsimd.memset(w[:, V:], 0.0)
 
+        if SUMMED_ON_TENSOR:
+            ident = keep.tile([P, P], F32, name="ident")
+            make_identity(nc, ident[:])
         ga_abs = keep.tile([P, PACK], F32, name="ga_abs")
         nc.scalar.activation(ga_abs[:], ga_t[:], ACT.Abs)
         ga_pos = keep.tile([P, PACK], F32, name="ga_pos")
-        nc.gpsimd.tensor_scalar(ga_pos[:], ga_t[:], 0.0, 2.0, ALU.is_ge, ALU.mult)
+        nc.gpsimd.tensor_scalar(ga_pos[:], ga_t[:], 0.0, -2.0, ALU.is_ge, ALU.mult)
         ga_sign = keep.tile([P, PACK], F32, name="ga_sign")
-        nc.gpsimd.tensor_scalar(ga_sign[:], ga_pos[:], -1.0, 1.0, ALU.add, ALU.mult)
+        nc.gpsimd.tensor_scalar(ga_sign[:], ga_pos[:], 1.0, 1.0, ALU.add, ALU.mult)
         gb_signed = keep.tile([P, PACK], F32, name="gb_signed")
         nc.gpsimd.tensor_tensor(gb_signed[:], gb_t[:], ga_sign[:], ALU.mult)
 
@@ -84,6 +89,11 @@ def tile_picked_kqbigtrimfoldd_none_p_kernel(tc, x_words, x_scales, w1, w2, ga, 
         def deal(copy, name, src, t, m0, m1):
             grouped = keep.tile([P, (m1 - m0) * PACK], BF16, name=name, align_bytes=64)
             copy(grouped[:].rearrange("p (m j) -> p m j", j=PACK), src[:].rearrange("p j (m t) -> p t m j", t=PACK)[:, t, m0:m1])
+            return grouped
+
+        def deal_many(name, src, t0):
+            grouped = keep.tile([P, (PACK - t0) * P * PACK], BF16, name=name, align_bytes=64)
+            nc.scalar.copy(grouped[:].rearrange("p (t m j) -> p m t j", m=P, j=PACK), src[:].rearrange("p j (m t) -> p m t j", t=PACK)[:, :, t0:])
             return grouped
 
         def quantise(held, col, grouped):
@@ -102,22 +112,24 @@ def tile_picked_kqbigtrimfoldd_none_p_kernel(tc, x_words, x_scales, w1, w2, ga, 
         x_b = mx_tiles("xb", V)
         x_a = mx_tiles("xa", S)
         nc.vector.tensor_copy(x_b[1][:], xs[:].indirect(l_two[:]))
-        w2q = [mx_tiles("w2q%d" % t, P) for t in range(PACK)]
-        w2g = [deal(nc.vector.tensor_copy, "w2g0", w2_raw, 0, 0, P)]
-        w2g.extend(deal(nc.scalar.copy, "w2g%d" % t, w2_raw, t, 0, P) for t in range(1, PACK))
+        w2q = [mx_tiles("w2q%d" % t, P) for t in range(2)]
+        w2g = [deal(nc.scalar.copy, "w2g%d" % t, w2_raw, t, 0, P) for t in range(2)]
+        w2_rest = deal_many("w2_rest", w2_raw, 2)
+        w2q_rest = mx_tiles("w2q_rest", 2 * P)
+        w2q[2:] = [(w2q_rest[0][:, i * P : (i + 1) * P], w2q_rest[1][:, i * P : (i + 1) * P]) for i in range(2)]
         nc.vector.tensor_copy(x_a[1][:], xs[:].indirect(l_offs[:]))
         quantise(w2q[0], 0, w2g[0])
         quantise(w2q[1], 0, w2g[1])
         for cols in halves:
             nc.vector.tensor_copy(x_b[0][:, cols], xw[:].indirect(l_two[:, cols.start // 16 : cols.stop // 16]))
         nc.vector.tensor_copy(x_a[0][:], xw[:].indirect(l_offs[:]))
-        quantise(w2q[2], 0, w2g[2])
-        quantise(w2q[3], 0, w2g[3])
+        quantise(w2q_rest, 0, w2_rest)
 
         def b_rows(j, bank, cols):
             acc = product(bank, w2q[j], x_b, cols)
-            nc.scalar.copy(win_b[j][:, cols], acc[:])
-            nc.scalar.copy(win_a[j][:, V + cols.start : V + cols.stop], acc[:])
+            nc.scalar.activation(win_b[j][:, cols], acc[:], ACT.Copy, scale=-1.0)
+            if j >= SUMMED_ON_TENSOR:
+                nc.scalar.activation(win_a[j][:, V + cols.start : V + cols.stop], acc[:], ACT.Copy, scale=-1.0)
 
         b_rows(0, 0, halves[0])
         b_rows(0, PACK, halves[1])
@@ -125,61 +137,101 @@ def tile_picked_kqbigtrimfoldd_none_p_kernel(tc, x_words, x_scales, w1, w2, ga, 
             b_rows(j, j, whole)
 
         z2_rows = keep.tile([P, PACK - 1, V], BF16, name="z2_rows")
-        z2_grouped = keep.tile([P, V * PACK], BF16, name="z2_grouped", align_bytes=64)
-        z2_slots = z2_grouped[:].rearrange("p (v j) -> p v j", j=PACK)
+        z2_all = keep.tile([P, V * PACK], BF16, name="z2_all", align_bytes=64)
+        z2_grouped = [z2_all[:, h * HALF * PACK : (h + 1) * HALF * PACK] for h in range(2)]
+        z2_slots = z2_all[:].rearrange("p (v j) -> p v j", j=PACK)
         z_rows = keep.tile([P, PACK, S], BF16, name="z_rows")
-        d3 = {}
-        d4 = {}
+        got3 = {}
+        got4 = {}
         top = {}
         a_acc = {}
         a_got = {}
+        a_own = [keep.tile([P, S], BF16, name="a_own%d" % j) for j in range(PACK)]
+
+        def z2_out(j, src):
+            gain = gb_signed[:, j : j + 1]
+            if j < PACK - 1:
+                nc.scalar.activation(z2_rows[:, j, :], src[:], ACT.Copy, scale=gain)
+            else:
+                nc.scalar.activation(z2_slots[:, :, j], src[:], ACT.Copy, scale=gain)
 
         def b_first(j):
-            d3[j] = ring.tile([P, V], F32, name="d3")
-            nc.vector.tensor_tensor(d3[j][:], win_b[j][:].indirect(l3[:]), win_a[j][:, V:], ALU.subtract)
+            got3[j] = ring.tile([P, V], F32, name="got3")
+            if j < SUMMED_ON_TENSOR:
+                nc.vector.tensor_copy(got3[j][:], win_b[j][:].indirect(l3[:]))
+            else:
+                nc.vector.tensor_tensor(got3[j][:], win_b[j][:].indirect(l3[:]), win_a[j][:, V:], ALU.subtract)
 
         def b_second(j):
-            d4[j] = ring.tile([P, V], F32, name="d4")
-            nc.vector.tensor_tensor(d4[j][:], win_b[j][:].indirect(l4[:]), win_a[j][:, V:], ALU.subtract)
+            got4[j] = ring.tile([P, V], F32, name="got4")
+            other = got3[j][:] if j < SUMMED_ON_TENSOR else win_a[j][:, V:]
+            nc.vector.tensor_tensor(got4[j][:], win_b[j][:].indirect(l4[:]), other, ALU.subtract)
 
         def b_top(j):
             top[j] = ring.tile([P, V], F32, name="top")
-            nc.vector.tensor_tensor(top[j][:], d3[j][:], d4[j][:], ALU.max)
+            if j < SUMMED_ON_TENSOR:
+                nc.scalar.activation(top[j][:], got4[j][:], ACT.Relu, scale=-1.0)
+            else:
+                nc.vector.tensor_tensor(top[j][:], got3[j][:], got4[j][:], ALU.min)
 
         def b_last(j):
-            z2f = ring.tile([P, V], F32, name="z2f")
-            nc.vector.tensor_tensor(z2f[:], win_b[j][:].indirect(l2[:]), top[j][:], ALU.subtract)
-            dst = z2_rows[:, j, :] if j < PACK - 1 else z2_slots[:, :, j]
-            nc.scalar.activation(dst, z2f[:], ACT.Copy, scale=gb_signed[:, j : j + 1])
+            if j >= SUMMED_ON_TENSOR:
+                z2f = ring.tile([P, V], F32, name="z2f")
+                nc.vector.tensor_tensor(z2f[:], win_b[j][:].indirect(l2[:]), top[j][:], ALU.subtract)
+                z2_out(j, z2f)
+                return
+            rest = win_a[j][:, V:]
+            nc.vector.tensor_tensor(rest, win_b[j][:].indirect(l2[:]), got3[j][:], ALU.subtract)
+            turned = psum.tile([P, V], F32, name="bank%d" % (j % 2))
+            terms = [win_b[j][:, :V], rest, top[j][:]]
+            for c in range(V // P):
+                cols = slice(c * P, (c + 1) * P)
+                for i, term in enumerate(terms):
+                    nc.tensor.matmul(turned[:, cols], lhsT=term[:, cols], rhs=ident[:], is_transpose=True, start=(i == 0), stop=(i == len(terms) - 1))
+            turned_sb = ring.tile([P, V], F32, name="turned_sb")
+            nc.scalar.copy(turned_sb[:], turned[:])
+            back = psum.tile([P, V], F32, name="bank%d" % (2 + j % 2))
+            for c in range(V // P):
+                cols = slice(c * P, (c + 1) * P)
+                nc.tensor.transpose(back[:, cols], turned_sb[:, cols], ident[:])
+            z2_out(j, back)
 
         def a_rows(j, stationary):
             a_acc[j] = product(PACK + j, stationary, x_a, whole)
             nc.scalar.activation(win_a[j][:, :S], a_acc[j][:], ACT.Copy, scale=ga_abs[:, j : j + 1])
 
+        def a_round(j):
+            nc.scalar.activation(a_own[j][:], a_acc[j][:], ACT.Copy, scale=ga_abs[:, j : j + 1])
+
         def a_gather(j):
-            a_got[j] = ring.tile([P, S], F32, name="a_got")
+            a_got[j] = ring.tile([P, S], BF16, name="a_got")
             nc.vector.tensor_copy(a_got[j][:], win_a[j][:].indirect(l1[:]))
 
         def a_top(j, cols):
-            nc.vector.scalar_tensor_tensor(z_rows[:, j, cols], a_acc[j][:, cols], ga_abs[:, j : j + 1], a_got[j][:, cols], ALU.mult, ALU.max)
+            nc.vector.tensor_tensor(z_rows[:, j, cols], a_own[j][:, cols], a_got[j][:, cols], ALU.max)
 
-        w1g = keep.tile([P, H * PACK], BF16, name="w1g", align_bytes=64)
         w1q = mx_tiles("w1q", H)
+        quantise(w1q, 0, deal_many("w1g", w1_raw, 0))
 
+        z2q = mx_tiles("z2q", V)
         b_first(0)
         b_second(0)
-        for j in range(1, PACK):
-            b_first(j)
-            b_top(j - 1)
-            b_second(j)
-            b_last(j - 1)
-            if j == 1:
-                for t in range(PACK):
-                    nc.scalar.copy(w1g[:, t * H : (t + 1) * H].rearrange("p (m j) -> p m j", j=PACK), w1_raw[:].rearrange("p j (m t) -> p t m j", t=PACK)[:, t])
-            if j == 2:
-                quantise(w1q, 0, w1g)
-                for i in range(PACK):
-                    a_rows(i, (w1q[0][:, i * P : (i + 1) * P], w1q[1][:, i * P : (i + 1) * P]))
+        b_first(1)
+        b_top(0)
+        b_second(1)
+        b_last(0)
+        b_first(2)
+        b_top(1)
+        for i in range(PACK):
+            a_rows(i, (w1q[0][:, i * P : (i + 1) * P], w1q[1][:, i * P : (i + 1) * P]))
+        b_second(2)
+        b_last(1)
+        b_first(3)
+        b_top(2)
+        b_second(3)
+        b_last(2)
+        for i in range(PACK):
+            a_round(i)
         nc.scalar.copy(z2_slots[:, :, : PACK - 1], z2_rows[:].rearrange("p j v -> p v j"))
         a_gather(0)
         b_top(3)
@@ -188,10 +240,10 @@ def tile_picked_kqbigtrimfoldd_none_p_kernel(tc, x_words, x_scales, w1, w2, ga, 
         a_top(0, whole)
         a_gather(2)
         a_top(1, whole)
-        z2q = mx_tiles("z2q", V)
-        quantise(z2q, 0, z2_grouped)
         a_gather(3)
         a_top(2, whole)
+        for h in range(2):
+            quantise(z2q, h * HALF, z2_grouped[h])
         for cols in halves:
             a_top(3, cols)
 
@@ -200,14 +252,13 @@ def tile_picked_kqbigtrimfoldd_none_p_kernel(tc, x_words, x_scales, w1, w2, ga, 
         zg3 = deal(nc.scalar.copy, "zg3", z_rows, 3, 0, P)
         for h in range(2):
             quantise(zq[0], h * P // 2, first[h])
-        zg1 = deal(nc.vector.tensor_copy, "zg1", z_rows, 1, 0, P)
-        zg2 = deal(nc.vector.tensor_copy, "zg2", z_rows, 2, 0, P)
-        quantise(zq[1], 0, zg1)
-        quantise(zq[2], 0, zg2)
-        quantise(zq[3], 0, zg3)
+        zg12 = keep.tile([P, 2 * P * PACK], BF16, name="z2_all", align_bytes=64)
+        nc.vector.tensor_copy(zg12[:].rearrange("p (t m j) -> p m t j", m=P, j=PACK), z_rows[:].rearrange("p j (m t) -> p m t j", t=PACK)[:, :, 1:3])
+        zq12 = mx_tiles("zq12", 2 * P)
+        zq[1:3] = [(zq12[0][:, i * P : (i + 1) * P], zq12[1][:, i * P : (i + 1) * P]) for i in range(2)]
 
         out_rows = out.rearrange("(p t) v -> t p v", t=PACK)
-        ds = [keep.tile([P, V], F32, name="ds%d" % t) for t in range(PACK)]
+        ds = {}
         s_acc = {}
         pa = {}
         pb = {}
@@ -215,9 +266,13 @@ def tile_picked_kqbigtrimfoldd_none_p_kernel(tc, x_words, x_scales, w1, w2, ga, 
         def s_rows(t, pieces):
             s_acc[t] = [(cols, product(bank, zq[t], z2q, cols)) for bank, cols in pieces]
             for cols, acc in s_acc[t]:
-                nc.scalar.activation(win_b[t][:, cols], acc[:], ACT.Copy, scale=0.0625)
+                if cols == halves[1]:
+                    nc.vector.tensor_scalar(win_b[t][:, cols], acc[:], 0.0625, None, ALU.mult)
+                else:
+                    nc.scalar.activation(win_b[t][:, cols], acc[:], ACT.Copy, scale=0.0625)
 
         def ds_base(t):
+            ds[t] = keep.tile([P, V], F32, name={0: "zq3_words", 3: "zq12_words"}.get(t, "ds%d" % t), align_bytes=64)
             for cols, acc in s_acc[t]:
                 nc.scalar.activation(ds[t][:, cols], acc[:], ACT.Copy, scale=0.0625)
 
@@ -241,18 +296,21 @@ def tile_picked_kqbigtrimfoldd_none_p_kernel(tc, x_words, x_scales, w1, w2, ga, 
                 nc.sync.dma_start(out_rows[t][:, cols], res[:])
 
         s_rows(0, [(0, halves[0]), (PACK, halves[1])])
+        quantise(zq12, 0, zg12)
+        quantise(zq[3], 0, zg3)
         pair_up(0)
-        for t in range(1, PACK):
-            s_rows(t, [(t, whole)])
-            ds_base(t - 1)
-            pair_up(t)
-            put_back(t - 1)
-            if t >= 2:
-                halve(t - 2)
-                finish(t - 2, [whole])
-        ds_base(3)
-        put_back(3)
-        halve(2)
-        finish(2, [whole])
-        halve(3)
-        finish(3, halves)
+        order = [0, 3, 1, 2]
+        for i in range(1, PACK):
+            s_rows(order[i], [(order[i], whole)])
+            ds_base(order[i - 1])
+            pair_up(order[i])
+            put_back(order[i - 1])
+            if i >= 2:
+                halve(order[i - 2])
+                finish(order[i - 2], [whole])
+        ds_base(order[3])
+        put_back(order[3])
+        halve(order[2])
+        finish(order[2], [whole])
+        halve(order[3])
+        finish(order[3], halves)

@@ -1,7 +1,6 @@
 from contextlib import ExitStack
 
 import concourse.mybir as mybir
-from concourse.masks import make_identity
 
 K, T, S, V, H, W = 512, 2048, 512, 512, 512, 256
 FLOPS = 2 * K * H * S + 2 * K * H * V + 2 * H * S * V
@@ -18,16 +17,22 @@ ACT = mybir.ActivationFunctionType
 
 P = 128
 PACK = 4
-WIN = 1024
-HALF = V // 2
-SUMMED_ON_TENSOR = 0
+LAST = PACK - 1
+LIST_ROWS = 16
+QUADRANT = 32
+WINDOW = 2 * V
+S_FACTOR = 0.0625
+PAIR_FACTOR = -0.5
+WHOLE = slice(0, V)
+HALVES = [slice(0, V // 2), slice(V // 2, V)]
+SPARE_BANK = PACK
 
 
 def tile_picked_kqbigtrimfoldd_none_p_kernel(tc, x_words, x_scales, w1, w2, ga, gb, offs, two, n1, n2, n3, n4, n5, n6, n7, out):
     nc = tc.nc
     with ExitStack() as ctx:
         keep = ctx.enter_context(tc.tile_pool(name="keep", bufs=1))
-        ring = ctx.enter_context(tc.tile_pool(name="ring", bufs=4))
+        per_tile = ctx.enter_context(tc.tile_pool(name="per_tile", bufs=PACK))
         psum = ctx.enter_context(tc.psum_pool(name="psum", bufs=1))
 
         def load_list(name, src):
@@ -47,13 +52,14 @@ def tile_picked_kqbigtrimfoldd_none_p_kernel(tc, x_words, x_scales, w1, w2, ga, 
 
         xs = keep.tile([P, T], U8, name="xs", align_bytes=64)
         nc.gpsimd.memset(xs[:].bitcast(I32), 0)
-        for q in range(4):
-            nc.scalar.dma_start(xs[32 * q : 32 * q + 4, :].bitcast(I32), x_scales[0, 4 * q : 4 * q + 4, :].bitcast(I32))
-        l_two = load_list("l_two", two)
+        for q in range(P // QUADRANT):
+            rows = x_scales[0, PACK * q : PACK * (q + 1), :]
+            nc.scalar.dma_start(xs[QUADRANT * q : QUADRANT * q + PACK, :].bitcast(I32), rows.bitcast(I32))
         l_offs = load_list("l_offs", offs)
-        w2_raw = load_weight("w2_raw", w2)
         xw = keep.tile([P, T], U32, name="xw", align_bytes=64)
-        nc.sync.dma_start(xw[:].bitcast(I32), x_words[0].rearrange("p n t -> p (n t)").bitcast(I32))
+        nc.sync.dma_start(xw[:].bitcast(I32), x_words[0].rearrange("p n r -> p (n r)").bitcast(I32))
+        l_two = load_list("l_two", two)
+        w2_raw = load_weight("w2_raw", w2)
         ga_t = load_gain("ga_t", ga)
         l3 = load_list("l3", n3)
         l4 = load_list("l4", n4)
@@ -65,252 +71,217 @@ def tile_picked_kqbigtrimfoldd_none_p_kernel(tc, x_words, x_scales, w1, w2, ga, 
         l6 = load_list("l6", n6)
         l7 = load_list("l7", n7)
 
-        win_b = [keep.tile([P, WIN], F32, name="win_b%d" % j) for j in range(PACK)]
-        win_a = [keep.tile([P, WIN], F32, name="win_a%d" % j) for j in range(PACK)]
-        for w in win_b:
-            nc.gpsimd.memset(w[:, V:], 0.0)
+        win_b = [keep.tile([P, WINDOW], F32, name="win_b%d" % t) for t in range(PACK)]
+        win_a = [keep.tile([P, WINDOW], F32, name="win_a%d" % t) for t in range(PACK)]
+        b_plain = [win[:, V:] for win in win_a]
+        for win in win_b:
+            nc.gpsimd.memset(win[:, V:], 0.0)
 
-        if SUMMED_ON_TENSOR:
-            ident = keep.tile([P, P], F32, name="ident")
-            make_identity(nc, ident[:])
         ga_abs = keep.tile([P, PACK], F32, name="ga_abs")
         nc.scalar.activation(ga_abs[:], ga_t[:], ACT.Abs)
-        ga_pos = keep.tile([P, PACK], F32, name="ga_pos")
-        nc.gpsimd.tensor_scalar(ga_pos[:], ga_t[:], 0.0, -2.0, ALU.is_ge, ALU.mult)
+        ga_step = keep.tile([P, PACK], F32, name="ga_step")
+        nc.gpsimd.tensor_scalar(ga_step[:], ga_t[:], 0.0, 2.0, ALU.is_ge, ALU.mult)
         ga_sign = keep.tile([P, PACK], F32, name="ga_sign")
-        nc.gpsimd.tensor_scalar(ga_sign[:], ga_pos[:], 1.0, 1.0, ALU.add, ALU.mult)
+        nc.gpsimd.tensor_scalar(ga_sign[:], ga_step[:], -1.0, 1.0, ALU.add, ALU.mult)
         gb_signed = keep.tile([P, PACK], F32, name="gb_signed")
         nc.gpsimd.tensor_tensor(gb_signed[:], gb_t[:], ga_sign[:], ALU.mult)
 
         def mx_tiles(name, width):
-            return (keep.tile([P, width], U32, name=name + "_words", align_bytes=64),
-                    keep.tile([P, width], U8, name=name + "_scales", align_bytes=64))
+            words = keep.tile([P, width], U32, name=name + "_words", align_bytes=64)
+            scales = keep.tile([P, width], U8, name=name + "_scales", align_bytes=64)
+            return words, scales
 
-        def deal(copy, name, src, t, m0, m1):
-            grouped = keep.tile([P, (m1 - m0) * PACK], BF16, name=name, align_bytes=64)
-            copy(grouped[:].rearrange("p (m j) -> p m j", j=PACK), src[:].rearrange("p j (m t) -> p t m j", t=PACK)[:, t, m0:m1])
-            return grouped
+        def stationary_tile(operand, i):
+            cols = slice(i * P, (i + 1) * P)
+            return operand[0][:, cols], operand[1][:, cols]
 
-        def deal_many(name, src, t0):
-            grouped = keep.tile([P, (PACK - t0) * P * PACK], BF16, name=name, align_bytes=64)
-            nc.scalar.copy(grouped[:].rearrange("p (t m j) -> p m t j", m=P, j=PACK), src[:].rearrange("p j (m t) -> p m t j", t=PACK)[:, :, t0:])
-            return grouped
+        def deal(copy, name, src, t, m0=0, m1=P):
+            dealt = keep.tile([P, (m1 - m0) * PACK], BF16, name=name, align_bytes=64)
+            view = src[:].rearrange("p j (m t) -> p t m j", t=PACK)[:, t, m0:m1]
+            copy(dealt[:].rearrange("p (m j) -> p m j", j=PACK), view)
+            return dealt
 
-        def quantise(held, col, grouped):
-            cols = slice(col, col + grouped.shape[1] // PACK)
-            nc.vector.quantize_mx(out=held[0][:, cols].bitcast(FP8X4), scales=held[1][:, cols], in_=grouped[:])
+        def deal_tiles(copy, name, src, t0, t1):
+            dealt = keep.tile([P, (t1 - t0) * P * PACK], BF16, name=name, align_bytes=64)
+            view = src[:].rearrange("p j (m t) -> p m t j", t=PACK)[:, :, t0:t1]
+            copy(dealt[:].rearrange("p (t m j) -> p m t j", m=P, j=PACK), view)
+            return dealt
+
+        def quantise(operand, first_col, grouped):
+            cols = slice(first_col, first_col + grouped.shape[1] // PACK)
+            nc.vector.quantize_mx(out=operand[0][:, cols].bitcast(FP8X4), scales=operand[1][:, cols], in_=grouped[:])
 
         def product(bank, stationary, moving, cols):
             acc = psum.tile([P, cols.stop - cols.start], F32, name="bank%d" % bank)
-            nc.tensor.matmul_mx(out=acc[:], lhsT=stationary[0][:].bitcast(FP8X4), lhsT_scale=stationary[1][:],
-                                rhs=moving[0][:, cols].bitcast(FP8X4), rhs_scale=moving[1][:, cols], start=True, stop=True)
+            nc.tensor.matmul_mx(
+                out=acc[:],
+                lhsT=stationary[0][:].bitcast(FP8X4),
+                lhsT_scale=stationary[1][:],
+                rhs=moving[0][:, cols].bitcast(FP8X4),
+                rhs_scale=moving[1][:, cols],
+                start=True,
+                stop=True,
+            )
             return acc
 
-        halves = [slice(0, HALF), slice(HALF, V)]
-        whole = slice(0, V)
-
         x_b = mx_tiles("xb", V)
-        x_a = mx_tiles("xa", S)
+        xa_words = keep.tile([P, S], U32, name="xa_words", align_bytes=64)
+        nc.vector.tensor_copy(xa_words[:], xw[:].indirect(l_offs[:]))
+        nc.vector.tensor_copy(x_b[0][:], xw[:].indirect(l_two[:]))
         nc.vector.tensor_copy(x_b[1][:], xs[:].indirect(l_two[:]))
-        w2q = [mx_tiles("w2q%d" % t, P) for t in range(2)]
-        w2g = [deal(nc.scalar.copy, "w2g%d" % t, w2_raw, t, 0, P) for t in range(2)]
-        w2_rest = deal_many("w2_rest", w2_raw, 2)
-        w2q_rest = mx_tiles("w2q_rest", 2 * P)
-        w2q[2:] = [(w2q_rest[0][:, i * P : (i + 1) * P], w2q_rest[1][:, i * P : (i + 1) * P]) for i in range(2)]
-        nc.vector.tensor_copy(x_a[1][:], xs[:].indirect(l_offs[:]))
-        quantise(w2q[0], 0, w2g[0])
-        quantise(w2q[1], 0, w2g[1])
-        for cols in halves:
-            nc.vector.tensor_copy(x_b[0][:, cols], xw[:].indirect(l_two[:, cols.start // 16 : cols.stop // 16]))
-        nc.vector.tensor_copy(x_a[0][:], xw[:].indirect(l_offs[:]))
-        quantise(w2q_rest, 0, w2_rest)
+        w2q = [mx_tiles("w2q%d" % t, P) for t in range(PACK)]
+        w2_dealt0 = deal(nc.scalar.copy, "w2_dealt0", w2_raw, 0)
+        w2_dealt1 = deal(nc.scalar.copy, "w2_dealt1", w2_raw, 1)
+        quantise(w2q[0], 0, w2_dealt0)
+        w2_dealt2 = deal(nc.vector.tensor_copy, "w2_dealt0", w2_raw, 2)
+        quantise(w2q[1], 0, w2_dealt1)
+        xa_scales = keep.tile([P, S], U8, name="w2_dealt1", align_bytes=64)
+        nc.vector.tensor_copy(xa_scales[:], xs[:].indirect(l_offs[:]))
+        x_a = (xa_words, xa_scales)
+        quantise(w2q[2], 0, w2_dealt2)
 
-        def b_rows(j, bank, cols):
-            acc = product(bank, w2q[j], x_b, cols)
-            nc.scalar.activation(win_b[j][:, cols], acc[:], ACT.Copy, scale=-1.0)
-            if j >= SUMMED_ON_TENSOR:
-                nc.scalar.activation(win_a[j][:, V + cols.start : V + cols.stop], acc[:], ACT.Copy, scale=-1.0)
+        def b_rows(t, bank, cols):
+            acc = product(bank, w2q[t], x_b, cols)
+            nc.scalar.copy(win_b[t][:, cols], acc[:])
+            nc.scalar.copy(b_plain[t][:, cols], acc[:])
 
-        b_rows(0, 0, halves[0])
-        b_rows(0, PACK, halves[1])
-        for j in range(1, PACK):
-            b_rows(j, j, whole)
+        b_rows(0, 0, HALVES[0])
+        b_rows(0, SPARE_BANK, HALVES[1])
+        for t in range(1, LAST):
+            b_rows(t, t, WHOLE)
+        quantise(w2q[LAST], 0, deal(nc.scalar.copy, "w2q1_words", w2_raw, LAST))
+        b_rows(LAST, LAST, WHOLE)
+        w1q = mx_tiles("w1q", H)
+        quantise(w1q, 0, deal_tiles(nc.scalar.copy, "w2q2_words", w1_raw, 0, PACK))
 
-        z2_rows = keep.tile([P, PACK - 1, V], BF16, name="z2_rows")
+        z2_rows = keep.tile([P, LAST, V], BF16, name="z2_rows")
         z2_all = keep.tile([P, V * PACK], BF16, name="z2_all", align_bytes=64)
-        z2_grouped = [z2_all[:, h * HALF * PACK : (h + 1) * HALF * PACK] for h in range(2)]
         z2_slots = z2_all[:].rearrange("p (v j) -> p v j", j=PACK)
         z_rows = keep.tile([P, PACK, S], BF16, name="z_rows")
-        got3 = {}
-        got4 = {}
-        top = {}
+        a_own = [keep.tile([P, S], BF16, name="a_own%d" % t) for t in range(PACK)]
+        less3 = {}
+        less4 = {}
+        larger = {}
         a_acc = {}
-        a_got = {}
-        a_own = [keep.tile([P, S], BF16, name="a_own%d" % j) for j in range(PACK)]
+        a_other = {}
 
-        def z2_out(j, src):
-            gain = gb_signed[:, j : j + 1]
-            if j < PACK - 1:
-                nc.scalar.activation(z2_rows[:, j, :], src[:], ACT.Copy, scale=gain)
-            else:
-                nc.scalar.activation(z2_slots[:, :, j], src[:], ACT.Copy, scale=gain)
+        def b_at_n3(t):
+            less3[t] = per_tile.tile([P, V], F32, name="less3")
+            nc.vector.tensor_tensor(less3[t][:], win_b[t][:].indirect(l3[:]), b_plain[t], ALU.subtract)
 
-        def b_first(j):
-            got3[j] = ring.tile([P, V], F32, name="got3")
-            if j < SUMMED_ON_TENSOR:
-                nc.vector.tensor_copy(got3[j][:], win_b[j][:].indirect(l3[:]))
-            else:
-                nc.vector.tensor_tensor(got3[j][:], win_b[j][:].indirect(l3[:]), win_a[j][:, V:], ALU.subtract)
+        def b_at_n4(t):
+            less4[t] = per_tile.tile([P, V], F32, name="less4")
+            nc.vector.tensor_tensor(less4[t][:], win_b[t][:].indirect(l4[:]), b_plain[t], ALU.subtract)
 
-        def b_second(j):
-            got4[j] = ring.tile([P, V], F32, name="got4")
-            other = got3[j][:] if j < SUMMED_ON_TENSOR else win_a[j][:, V:]
-            nc.vector.tensor_tensor(got4[j][:], win_b[j][:].indirect(l4[:]), other, ALU.subtract)
+        def b_larger(t):
+            larger[t] = per_tile.tile([P, V], F32, name="larger")
+            nc.vector.tensor_tensor(larger[t][:], less3[t][:], less4[t][:], ALU.max)
 
-        def b_top(j):
-            top[j] = ring.tile([P, V], F32, name="top")
-            if j < SUMMED_ON_TENSOR:
-                nc.scalar.activation(top[j][:], got4[j][:], ACT.Relu, scale=-1.0)
-            else:
-                nc.vector.tensor_tensor(top[j][:], got3[j][:], got4[j][:], ALU.min)
+        def b_at_n2(t):
+            unweighted = per_tile.tile([P, V], F32, name="unweighted")
+            nc.vector.tensor_tensor(unweighted[:], win_b[t][:].indirect(l2[:]), larger[t][:], ALU.subtract)
+            rounded = z2_rows[:, t, :] if t < LAST else z2_slots[:, :, LAST]
+            nc.scalar.activation(rounded, unweighted[:], ACT.Copy, scale=gb_signed[:, t : t + 1])
 
-        def b_last(j):
-            if j >= SUMMED_ON_TENSOR:
-                z2f = ring.tile([P, V], F32, name="z2f")
-                nc.vector.tensor_tensor(z2f[:], win_b[j][:].indirect(l2[:]), top[j][:], ALU.subtract)
-                z2_out(j, z2f)
-                return
-            rest = win_a[j][:, V:]
-            nc.vector.tensor_tensor(rest, win_b[j][:].indirect(l2[:]), got3[j][:], ALU.subtract)
-            turned = psum.tile([P, V], F32, name="bank%d" % (j % 2))
-            terms = [win_b[j][:, :V], rest, top[j][:]]
-            for c in range(V // P):
-                cols = slice(c * P, (c + 1) * P)
-                for i, term in enumerate(terms):
-                    nc.tensor.matmul(turned[:, cols], lhsT=term[:, cols], rhs=ident[:], is_transpose=True, start=(i == 0), stop=(i == len(terms) - 1))
-            turned_sb = ring.tile([P, V], F32, name="turned_sb")
-            nc.scalar.copy(turned_sb[:], turned[:])
-            back = psum.tile([P, V], F32, name="bank%d" % (2 + j % 2))
-            for c in range(V // P):
-                cols = slice(c * P, (c + 1) * P)
-                nc.tensor.transpose(back[:, cols], turned_sb[:, cols], ident[:])
-            z2_out(j, back)
+        def a_rows(t):
+            a_acc[t] = product(PACK + t, stationary_tile(w1q, t), x_a, WHOLE)
+            nc.scalar.activation(win_a[t][:, :S], a_acc[t][:], ACT.Copy, scale=ga_abs[:, t : t + 1])
 
-        def a_rows(j, stationary):
-            a_acc[j] = product(PACK + j, stationary, x_a, whole)
-            nc.scalar.activation(win_a[j][:, :S], a_acc[j][:], ACT.Copy, scale=ga_abs[:, j : j + 1])
+        def a_round(t):
+            nc.scalar.activation(a_own[t][:], a_acc[t][:], ACT.Copy, scale=ga_abs[:, t : t + 1])
 
-        def a_round(j):
-            nc.scalar.activation(a_own[j][:], a_acc[j][:], ACT.Copy, scale=ga_abs[:, j : j + 1])
+        def a_at_n1(t):
+            a_other[t] = per_tile.tile([P, S], BF16, name="a_other")
+            nc.vector.tensor_copy(a_other[t][:], win_a[t][:].indirect(l1[:]))
 
-        def a_gather(j):
-            a_got[j] = ring.tile([P, S], BF16, name="a_got")
-            nc.vector.tensor_copy(a_got[j][:], win_a[j][:].indirect(l1[:]))
-
-        def a_top(j, cols):
-            nc.vector.tensor_tensor(z_rows[:, j, cols], a_own[j][:, cols], a_got[j][:, cols], ALU.max)
-
-        w1q = mx_tiles("w1q", H)
-        quantise(w1q, 0, deal_many("w1g", w1_raw, 0))
+        def a_larger(t, cols):
+            nc.vector.tensor_tensor(z_rows[:, t, cols], a_own[t][:, cols], a_other[t][:, cols], ALU.max)
 
         z2q = mx_tiles("z2q", V)
-        b_first(0)
-        b_second(0)
-        b_first(1)
-        b_top(0)
-        b_second(1)
-        b_last(0)
-        b_first(2)
-        b_top(1)
-        for i in range(PACK):
-            a_rows(i, (w1q[0][:, i * P : (i + 1) * P], w1q[1][:, i * P : (i + 1) * P]))
-        b_second(2)
-        b_last(1)
-        b_first(3)
-        b_top(2)
-        b_second(3)
-        b_last(2)
-        for i in range(PACK):
-            a_round(i)
-        nc.scalar.copy(z2_slots[:, :, : PACK - 1], z2_rows[:].rearrange("p j v -> p v j"))
-        a_gather(0)
-        b_top(3)
-        a_gather(1)
-        b_last(3)
-        a_top(0, whole)
-        a_gather(2)
-        a_top(1, whole)
-        a_gather(3)
-        a_top(2, whole)
-        for h in range(2):
-            quantise(z2q, h * HALF, z2_grouped[h])
-        for cols in halves:
-            a_top(3, cols)
+        b_at_n3(0)
+        b_at_n4(0)
+        for t in range(1, PACK):
+            b_at_n3(t)
+            b_larger(t - 1)
+            if t == PACK // 2:
+                for i in range(PACK):
+                    a_rows(i)
+            b_at_n4(t)
+            b_at_n2(t - 1)
+        for t in range(PACK):
+            a_round(t)
+        nc.scalar.copy(z2_slots[:, :, :LAST], z2_rows[:].rearrange("p j v -> p v j"))
+        a_at_n1(0)
+        b_larger(LAST)
+        a_at_n1(1)
+        b_at_n2(LAST)
+        a_larger(0, WHOLE)
+        for t in range(2, PACK):
+            a_at_n1(t)
+            a_larger(t - 1, WHOLE)
+        for cols in HALVES:
+            quantise(z2q, cols.start, z2_all[:, cols.start * PACK : cols.stop * PACK])
 
-        zq = [mx_tiles("zq%d" % t, P) for t in range(PACK)]
-        first = [deal(nc.vector.tensor_copy, "zg0_%d" % h, z_rows, 0, h * P // 2, (h + 1) * P // 2) for h in range(2)]
-        zg3 = deal(nc.scalar.copy, "zg3", z_rows, 3, 0, P)
+        for cols in HALVES:
+            a_larger(LAST, cols)
+        zq_first = mx_tiles("zq_first", P)
+        zq_last = mx_tiles("zq_last", P)
+        z_dealt_first = [deal(nc.vector.tensor_copy, "z_dealt0_%d" % m0, z_rows, 0, m0, m0 + P // 2) for m0 in (0, P // 2)]
+        z_dealt_last = deal(nc.scalar.copy, "z_dealt3", z_rows, LAST)
         for h in range(2):
-            quantise(zq[0], h * P // 2, first[h])
-        zg12 = keep.tile([P, 2 * P * PACK], BF16, name="z2_all", align_bytes=64)
-        nc.vector.tensor_copy(zg12[:].rearrange("p (t m j) -> p m t j", m=P, j=PACK), z_rows[:].rearrange("p j (m t) -> p m t j", t=PACK)[:, :, 1:3])
-        zq12 = mx_tiles("zq12", 2 * P)
-        zq[1:3] = [(zq12[0][:, i * P : (i + 1) * P], zq12[1][:, i * P : (i + 1) * P]) for i in range(2)]
+            quantise(zq_first, h * P // 2, z_dealt_first[h])
+        z_dealt_middle = deal_tiles(nc.vector.tensor_copy, "z2_all", z_rows, 1, LAST)
+        zq_middle = mx_tiles("zq_middle", 2 * P)
+        zq = [zq_first, stationary_tile(zq_middle, 0), stationary_tile(zq_middle, 1), zq_last]
 
         out_rows = out.rearrange("(p t) v -> t p v", t=PACK)
-        ds = {}
         s_acc = {}
+        ds = {}
         pa = {}
-        pb = {}
+        pb_part = {}
 
-        def s_rows(t, pieces):
-            s_acc[t] = [(cols, product(bank, zq[t], z2q, cols)) for bank, cols in pieces]
-            for cols, acc in s_acc[t]:
-                if cols == halves[1]:
-                    nc.vector.tensor_scalar(win_b[t][:, cols], acc[:], 0.0625, None, ALU.mult)
-                else:
-                    nc.scalar.activation(win_b[t][:, cols], acc[:], ACT.Copy, scale=0.0625)
+        def s_rows(t):
+            s_acc[t] = [(WHOLE, product(t, zq[t], z2q, WHOLE))]
+            nc.scalar.activation(win_b[t][:, :V], s_acc[t][0][1][:], ACT.Copy, scale=S_FACTOR)
 
-        def ds_base(t):
-            ds[t] = keep.tile([P, V], F32, name={0: "zq3_words", 3: "zq12_words"}.get(t, "ds%d" % t), align_bytes=64)
+        def ds_base(t, name):
+            ds[t] = keep.tile([P, V], F32, name=name, align_bytes=64)
             for cols, acc in s_acc[t]:
-                nc.scalar.activation(ds[t][:, cols], acc[:], ACT.Copy, scale=0.0625)
+                nc.scalar.activation(ds[t][:, cols], acc[:], ACT.Copy, scale=S_FACTOR)
 
         def pair_up(t):
-            pa[t] = ring.tile([P, W], F32, name="pa")
+            pa[t] = per_tile.tile([P, W], F32, name="pa")
             nc.vector.tensor_copy(pa[t][:], win_b[t][:].indirect(l5[:]))
-            pb[t] = ring.tile([P, W], F32, name="pb")
-            nc.vector.tensor_scalar(pb[t][:], win_b[t][:].indirect(l6[:]), -0.5, 0.0, ALU.mult, ALU.add)
+            pb_part[t] = per_tile.tile([P, W], F32, name="pb_part")
+            nc.vector.tensor_scalar(pb_part[t][:], win_b[t][:].indirect(l6[:]), PAIR_FACTOR, 0.0, ALU.mult, ALU.add)
 
         def put_back(t):
-            nc.vector.tensor_tensor(ds[t][:].indirect(l6[:]), pa[t][:], pb[t][:], ALU.add)
-
-        def halve(t):
-            nc.scalar.activation(win_a[t][:, :V], ds[t][:], ACT.Copy, scale=-0.5)
+            nc.vector.tensor_tensor(ds[t][:].indirect(l6[:]), pa[t][:], pb_part[t][:], ALU.add)
 
         def finish(t, pieces):
+            nc.scalar.activation(win_a[t][:, :V], ds[t][:], ACT.Copy, scale=PAIR_FACTOR)
             for cols in pieces:
-                res = keep.tile([P, cols.stop - cols.start], F32, name="res%d_%d" % (t, cols.start))
-                entries = l7[:, cols.start // 16 : cols.stop // 16]
-                nc.vector.tensor_tensor(res[:], win_a[t][:].indirect(entries), ds[t][:, cols], ALU.add)
-                nc.sync.dma_start(out_rows[t][:, cols], res[:])
+                result = keep.tile([P, cols.stop - cols.start], F32, name="result%d_%d" % (t, cols.start))
+                entries = l7[:, cols.start // LIST_ROWS : cols.stop // LIST_ROWS]
+                nc.vector.tensor_tensor(result[:], win_a[t][:].indirect(entries), ds[t][:, cols], ALU.add)
+                nc.sync.dma_start(out_rows[t][:, cols], result[:])
 
-        s_rows(0, [(0, halves[0]), (PACK, halves[1])])
-        quantise(zq12, 0, zg12)
-        quantise(zq[3], 0, zg3)
+        s_acc[0] = [(cols, product(bank, zq[0], z2q, cols)) for bank, cols in zip((0, SPARE_BANK), HALVES)]
+        nc.scalar.activation(win_b[0][:, HALVES[0]], s_acc[0][0][1][:], ACT.Copy, scale=S_FACTOR)
+        nc.vector.tensor_scalar(win_b[0][:, HALVES[1]], s_acc[0][1][1][:], S_FACTOR, None, ALU.mult)
+        quantise(zq_middle, 0, z_dealt_middle)
+        quantise(zq_last, 0, z_dealt_last)
         pair_up(0)
-        order = [0, 3, 1, 2]
-        for i in range(1, PACK):
-            s_rows(order[i], [(order[i], whole)])
-            ds_base(order[i - 1])
-            pair_up(order[i])
+
+        order = [0, LAST, 1, 2]
+        ds_names = ["zq_last_words", "zq_middle_words", "ds_third", "ds_fourth"]
+        for i in range(1, PACK + 1):
+            if i < PACK:
+                s_rows(order[i])
+            ds_base(order[i - 1], ds_names[i - 1])
+            if i < PACK:
+                pair_up(order[i])
             put_back(order[i - 1])
             if i >= 2:
-                halve(order[i - 2])
-                finish(order[i - 2], [whole])
-        ds_base(order[3])
-        put_back(order[3])
-        halve(order[2])
-        finish(order[2], [whole])
-        halve(order[3])
-        finish(order[3], halves)
+                finish(order[i - 2], [WHOLE])
+        finish(order[LAST], HALVES)

@@ -47,7 +47,7 @@ def tile_picked_kqbigtrimfoldd_none_p_kernel(tc, x_words, x_scales, w1, w2, ga, 
 
         def load_gain(name, src):
             held = keep.tile([P, PACK], F32, name=name)
-            nc.sync.dma_start(held[:], src.rearrange("(p t) o -> p (t o)", t=PACK))
+            nc.gpsimd.dma_start(held[:], src.rearrange("(p t) o -> p (t o)", t=PACK))
             return held
 
         xs = keep.tile([P, T], U8, name="xs", align_bytes=64)
@@ -55,18 +55,18 @@ def tile_picked_kqbigtrimfoldd_none_p_kernel(tc, x_words, x_scales, w1, w2, ga, 
         for q in range(P // QUADRANT):
             rows = x_scales[0, PACK * q : PACK * (q + 1), :]
             nc.scalar.dma_start(xs[QUADRANT * q : QUADRANT * q + PACK, :].bitcast(I32), rows.bitcast(I32))
+        ga_t = load_gain("ga_t", ga)
+        gb_t = load_gain("gb_t", gb)
         l_offs = load_list("l_offs", offs)
         xw = keep.tile([P, T], U32, name="xw", align_bytes=64)
         nc.sync.dma_start(xw[:].bitcast(I32), x_words[0].rearrange("p n r -> p (n r)").bitcast(I32))
         l_two = load_list("l_two", two)
         w2_raw = load_weight("w2_raw", w2)
-        ga_t = load_gain("ga_t", ga)
         l3 = load_list("l3", n3)
         l4 = load_list("l4", n4)
         l2 = load_list("l2", n2)
-        w1_raw = load_weight("w1_raw", w1)
-        gb_t = load_gain("gb_t", gb)
         l1 = load_list("l1", n1)
+        w1_raw = load_weight("w1_raw", w1)
         l5 = load_list("l5", n5)
         l6 = load_list("l6", n6)
         l7 = load_list("l7", n7)

from contextlib import ExitStack

import concourse.mybir as mybir

K, T, S, V, H, W = 512, 2048, 512, 512, 512, 256
FLOPS = 2 * K * H * S + 2 * K * H * V + 2 * H * S * V

F32 = mybir.dt.float32
BF16 = mybir.dt.bfloat16
I32 = mybir.dt.int32
U32 = mybir.dt.uint32
U16 = mybir.dt.uint16
U8 = mybir.dt.uint8
FP8X4 = mybir.dt.float8_e4m3fn_x4
ALU = mybir.AluOpType
ACT = mybir.ActivationFunctionType

P = 128
PACK = 4
LAST = PACK - 1
LIST_ROWS = 16
QUADRANT = 32
WINDOW = 2 * V
S_FACTOR = 0.0625
PAIR_FACTOR = -0.5
WHOLE = slice(0, V)
HALVES = [slice(0, V // 2), slice(V // 2, V)]
SPARE_BANK = PACK


def tile_picked_kqbigtrimfoldd_none_p_kernel(tc, x_words, x_scales, w1, w2, ga, gb, offs, two, n1, n2, n3, n4, n5, n6, n7, out):
    nc = tc.nc
    with ExitStack() as ctx:
        keep = ctx.enter_context(tc.tile_pool(name="keep", bufs=1))
        per_tile = ctx.enter_context(tc.tile_pool(name="per_tile", bufs=PACK))
        psum = ctx.enter_context(tc.psum_pool(name="psum", bufs=1))

        def load_list(name, src):
            held = keep.tile([P, src.shape[1]], U16, name=name)
            nc.sync.dma_start(held[:], src)
            return held

        def load_weight(name, src):
            held = keep.tile([P, PACK, H], F32, name=name)
            nc.sync.dma_start(held[:], src.rearrange("(p j) c -> p j c", j=PACK))
            return held

        def load_gain(name, src):
            held = keep.tile([P, PACK], F32, name=name)
            nc.gpsimd.dma_start(held[:], src.rearrange("(p t) o -> p (t o)", t=PACK))
            return held

        xs = keep.tile([P, T], U8, name="xs", align_bytes=64)
        nc.gpsimd.memset(xs[:].bitcast(I32), 0)
        for q in range(P // QUADRANT):
            rows = x_scales[0, PACK * q : PACK * (q + 1), :]
            nc.scalar.dma_start(xs[QUADRANT * q : QUADRANT * q + PACK, :].bitcast(I32), rows.bitcast(I32))
        ga_t = load_gain("ga_t", ga)
        gb_t = load_gain("gb_t", gb)
        l_offs = load_list("l_offs", offs)
        xw = keep.tile([P, T], U32, name="xw", align_bytes=64)
        nc.sync.dma_start(xw[:].bitcast(I32), x_words[0].rearrange("p n r -> p (n r)").bitcast(I32))
        l_two = load_list("l_two", two)
        w2_raw = load_weight("w2_raw", w2)
        l3 = load_list("l3", n3)
        l4 = load_list("l4", n4)
        l2 = load_list("l2", n2)
        l1 = load_list("l1", n1)
        w1_raw = load_weight("w1_raw", w1)
        l5 = load_list("l5", n5)
        l6 = load_list("l6", n6)
        l7 = load_list("l7", n7)

        win_b = [keep.tile([P, WINDOW], F32, name="win_b%d" % t) for t in range(PACK)]
        win_a = [keep.tile([P, WINDOW], F32, name="win_a%d" % t) for t in range(PACK)]
        b_plain = [win[:, V:] for win in win_a]
        for win in win_b:
            nc.gpsimd.memset(win[:, V:], 0.0)

        ga_abs = keep.tile([P, PACK], F32, name="ga_abs")
        nc.scalar.activation(ga_abs[:], ga_t[:], ACT.Abs)
        ga_step = keep.tile([P, PACK], F32, name="ga_step")
        nc.gpsimd.tensor_scalar(ga_step[:], ga_t[:], 0.0, 2.0, ALU.is_ge, ALU.mult)
        ga_sign = keep.tile([P, PACK], F32, name="ga_sign")
        nc.gpsimd.tensor_scalar(ga_sign[:], ga_step[:], -1.0, 1.0, ALU.add, ALU.mult)
        gb_signed = keep.tile([P, PACK], F32, name="gb_signed")
        nc.gpsimd.tensor_tensor(gb_signed[:], gb_t[:], ga_sign[:], ALU.mult)

        def mx_tiles(name, width):
            words = keep.tile([P, width], U32, name=name + "_words", align_bytes=64)
            scales = keep.tile([P, width], U8, name=name + "_scales", align_bytes=64)
            return words, scales

        def stationary_tile(operand, i):
            cols = slice(i * P, (i + 1) * P)
            return operand[0][:, cols], operand[1][:, cols]

        def deal(copy, name, src, t, m0=0, m1=P):
            dealt = keep.tile([P, (m1 - m0) * PACK], BF16, name=name, align_bytes=64)
            view = src[:].rearrange("p j (m t) -> p t m j", t=PACK)[:, t, m0:m1]
            copy(dealt[:].rearrange("p (m j) -> p m j", j=PACK), view)
            return dealt

        def deal_tiles(copy, name, src, t0, t1):
            dealt = keep.tile([P, (t1 - t0) * P * PACK], BF16, name=name, align_bytes=64)
            view = src[:].rearrange("p j (m t) -> p m t j", t=PACK)[:, :, t0:t1]
            copy(dealt[:].rearrange("p (t m j) -> p m t j", m=P, j=PACK), view)
            return dealt

        def quantise(operand, first_col, grouped):
            cols = slice(first_col, first_col + grouped.shape[1] // PACK)
            nc.vector.quantize_mx(out=operand[0][:, cols].bitcast(FP8X4), scales=operand[1][:, cols], in_=grouped[:])

        def product(bank, stationary, moving, cols):
            acc = psum.tile([P, cols.stop - cols.start], F32, name="bank%d" % bank)
            nc.tensor.matmul_mx(
                out=acc[:],
                lhsT=stationary[0][:].bitcast(FP8X4),
                lhsT_scale=stationary[1][:],
                rhs=moving[0][:, cols].bitcast(FP8X4),
                rhs_scale=moving[1][:, cols],
                start=True,
                stop=True,
            )
            return acc

        x_b = mx_tiles("xb", V)
        xa_words = keep.tile([P, S], U32, name="xa_words", align_bytes=64)
        nc.vector.tensor_copy(xa_words[:], xw[:].indirect(l_offs[:]))
        nc.vector.tensor_copy(x_b[0][:], xw[:].indirect(l_two[:]))
        nc.vector.tensor_copy(x_b[1][:], xs[:].indirect(l_two[:]))
        w2q = [mx_tiles("w2q%d" % t, P) for t in range(PACK)]
        w2_dealt0 = deal(nc.scalar.copy, "w2_dealt0", w2_raw, 0)
        w2_dealt1 = deal(nc.scalar.copy, "w2_dealt1", w2_raw, 1)
        quantise(w2q[0], 0, w2_dealt0)
        w2_dealt2 = deal(nc.vector.tensor_copy, "w2_dealt0", w2_raw, 2)
        quantise(w2q[1], 0, w2_dealt1)
        xa_scales = keep.tile([P, S], U8, name="w2_dealt1", align_bytes=64)
        nc.vector.tensor_copy(xa_scales[:], xs[:].indirect(l_offs[:]))
        x_a = (xa_words, xa_scales)
        quantise(w2q[2], 0, w2_dealt2)

        def b_rows(t, bank, cols):
            acc = product(bank, w2q[t], x_b, cols)
            nc.scalar.copy(win_b[t][:, cols], acc[:])
            nc.scalar.copy(b_plain[t][:, cols], acc[:])

        b_rows(0, 0, HALVES[0])
        b_rows(0, SPARE_BANK, HALVES[1])
        for t in range(1, LAST):
            b_rows(t, t, WHOLE)
        quantise(w2q[LAST], 0, deal(nc.scalar.copy, "w2q1_words", w2_raw, LAST))
        b_rows(LAST, LAST, WHOLE)
        w1q = mx_tiles("w1q", H)
        quantise(w1q, 0, deal_tiles(nc.scalar.copy, "w2q2_words", w1_raw, 0, PACK))

        z2_rows = keep.tile([P, LAST, V], BF16, name="z2_rows")
        z2_all = keep.tile([P, V * PACK], BF16, name="z2_all", align_bytes=64)
        z2_slots = z2_all[:].rearrange("p (v j) -> p v j", j=PACK)
        z_rows = keep.tile([P, PACK, S], BF16, name="z_rows")
        a_own = [keep.tile([P, S], BF16, name="a_own%d" % t) for t in range(PACK)]
        less3 = {}
        less4 = {}
        larger = {}
        a_acc = {}
        a_other = {}

        def b_at_n3(t):
            less3[t] = per_tile.tile([P, V], F32, name="less3")
            nc.vector.tensor_tensor(less3[t][:], win_b[t][:].indirect(l3[:]), b_plain[t], ALU.subtract)

        def b_at_n4(t):
            less4[t] = per_tile.tile([P, V], F32, name="less4")
            nc.vector.tensor_tensor(less4[t][:], win_b[t][:].indirect(l4[:]), b_plain[t], ALU.subtract)

        def b_larger(t):
            larger[t] = per_tile.tile([P, V], F32, name="larger")
            nc.vector.tensor_tensor(larger[t][:], less3[t][:], less4[t][:], ALU.max)

        def b_at_n2(t):
            unweighted = per_tile.tile([P, V], F32, name="unweighted")
            nc.vector.tensor_tensor(unweighted[:], win_b[t][:].indirect(l2[:]), larger[t][:], ALU.subtract)
            rounded = z2_rows[:, t, :] if t < LAST else z2_slots[:, :, LAST]
            nc.scalar.activation(rounded, unweighted[:], ACT.Copy, scale=gb_signed[:, t : t + 1])

        def a_rows(t):
            a_acc[t] = product(PACK + t, stationary_tile(w1q, t), x_a, WHOLE)
            nc.scalar.activation(win_a[t][:, :S], a_acc[t][:], ACT.Copy, scale=ga_abs[:, t : t + 1])

        def a_round(t):
            nc.scalar.activation(a_own[t][:], a_acc[t][:], ACT.Copy, scale=ga_abs[:, t : t + 1])

        def a_at_n1(t):
            a_other[t] = per_tile.tile([P, S], BF16, name="a_other")
            nc.vector.tensor_copy(a_other[t][:], win_a[t][:].indirect(l1[:]))

        def a_larger(t, cols):
            nc.vector.tensor_tensor(z_rows[:, t, cols], a_own[t][:, cols], a_other[t][:, cols], ALU.max)

        z2q = mx_tiles("z2q", V)
        b_at_n3(0)
        b_at_n4(0)
        for t in range(1, PACK):
            b_at_n3(t)
            b_larger(t - 1)
            if t == PACK // 2:
                for i in range(PACK):
                    a_rows(i)
            b_at_n4(t)
            b_at_n2(t - 1)
        for t in range(PACK):
            a_round(t)
        nc.scalar.copy(z2_slots[:, :, :LAST], z2_rows[:].rearrange("p j v -> p v j"))
        a_at_n1(0)
        b_larger(LAST)
        a_at_n1(1)
        b_at_n2(LAST)
        a_larger(0, WHOLE)
        for t in range(2, PACK):
            a_at_n1(t)
            a_larger(t - 1, WHOLE)
        for cols in HALVES:
            quantise(z2q, cols.start, z2_all[:, cols.start * PACK : cols.stop * PACK])

        for cols in HALVES:
            a_larger(LAST, cols)
        zq_first = mx_tiles("zq_first", P)
        zq_last = mx_tiles("zq_last", P)
        z_dealt_first = [deal(nc.vector.tensor_copy, "z_dealt0_%d" % m0, z_rows, 0, m0, m0 + P // 2) for m0 in (0, P // 2)]
        z_dealt_last = deal(nc.scalar.copy, "z_dealt3", z_rows, LAST)
        for h in range(2):
            quantise(zq_first, h * P // 2, z_dealt_first[h])
        z_dealt_middle = deal_tiles(nc.vector.tensor_copy, "z2_all", z_rows, 1, LAST)
        zq_middle = mx_tiles("zq_middle", 2 * P)
        zq = [zq_first, stationary_tile(zq_middle, 0), stationary_tile(zq_middle, 1), zq_last]

        out_rows = out.rearrange("(p t) v -> t p v", t=PACK)
        s_acc = {}
        ds = {}
        pa = {}
        pb_part = {}

        def s_rows(t):
            s_acc[t] = [(WHOLE, product(t, zq[t], z2q, WHOLE))]
            nc.scalar.activation(win_b[t][:, :V], s_acc[t][0][1][:], ACT.Copy, scale=S_FACTOR)

        def ds_base(t, name):
            ds[t] = keep.tile([P, V], F32, name=name, align_bytes=64)
            for cols, acc in s_acc[t]:
                nc.scalar.activation(ds[t][:, cols], acc[:], ACT.Copy, scale=S_FACTOR)

        def pair_up(t):
            pa[t] = per_tile.tile([P, W], F32, name="pa")
            nc.vector.tensor_copy(pa[t][:], win_b[t][:].indirect(l5[:]))
            pb_part[t] = per_tile.tile([P, W], F32, name="pb_part")
            nc.vector.tensor_scalar(pb_part[t][:], win_b[t][:].indirect(l6[:]), PAIR_FACTOR, 0.0, ALU.mult, ALU.add)

        def put_back(t):
            nc.vector.tensor_tensor(ds[t][:].indirect(l6[:]), pa[t][:], pb_part[t][:], ALU.add)

        def finish(t, pieces):
            nc.scalar.activation(win_a[t][:, :V], ds[t][:], ACT.Copy, scale=PAIR_FACTOR)
            for cols in pieces:
                result = keep.tile([P, cols.stop - cols.start], F32, name="result%d_%d" % (t, cols.start))
                entries = l7[:, cols.start // LIST_ROWS : cols.stop // LIST_ROWS]
                nc.vector.tensor_tensor(result[:], win_a[t][:].indirect(entries), ds[t][:, cols], ALU.add)
                nc.sync.dma_start(out_rows[t][:, cols], result[:])

        s_acc[0] = [(cols, product(bank, zq[0], z2q, cols)) for bank, cols in zip((0, SPARE_BANK), HALVES)]
        nc.scalar.activation(win_b[0][:, HALVES[0]], s_acc[0][0][1][:], ACT.Copy, scale=S_FACTOR)
        nc.vector.tensor_scalar(win_b[0][:, HALVES[1]], s_acc[0][1][1][:], S_FACTOR, None, ALU.mult)
        quantise(zq_middle, 0, z_dealt_middle)
        quantise(zq_last, 0, z_dealt_last)
        pair_up(0)

        order = [0, LAST, 1, 2]
        ds_names = ["zq_last_words", "zq_middle_words", "ds_third", "ds_fourth"]
        for i in range(1, PACK + 1):
            if i < PACK:
                s_rows(order[i])
            ds_base(order[i - 1], ds_names[i - 1])
            if i < PACK:
                pair_up(order[i])
            put_back(order[i - 1])
            if i >= 2:
                finish(order[i - 2], [WHOLE])
        finish(order[LAST], HALVES)
